import numpy as np
import ml_dtypes


def mxq(x, axis, fmt="e4m3"):
    dtype, down = {"e4m3": (ml_dtypes.float8_e4m3fn, 7), "e5m2": (ml_dtypes.float8_e5m2, 14)}[fmt]
    v = np.moveaxis(np.asarray(x, np.float32).astype(ml_dtypes.bfloat16).astype(np.float64), axis, -1)
    blocks = v.reshape(v.shape[:-1] + (-1, 32))
    amax = np.abs(blocks).max(-1, keepdims=True)
    byte = np.maximum(np.where(amax > 0, np.frexp(amax)[1] - 1 + 127, 0) - down, 1)
    scale = np.exp2(byte - 127.0)
    codes = (blocks / scale).astype(np.float32).astype(dtype).astype(np.float64)
    return np.moveaxis((codes * scale).reshape(v.shape), -1, axis)


WIDE = False


def mx_kscale(k):
    if not WIDE:
        return np.ones(k)
    levels = np.array([10, -10, 5, -5, 0])
    if k % 512:
        return np.exp2(np.random.permutation(np.resize(levels, k // 32))).repeat(32)
    a = np.empty((k // 512, 16))
    for p in range(k // 512):
        a[p, :8] = np.random.permutation(np.resize(levels, 8))
        for g in range(8):
            far = levels[np.abs(levels - a[p, g]) >= 10]
            a[p, g + 8] = far[np.random.randint(len(far))]
    return np.exp2(a.ravel()).repeat(32)


def f64(x):
    return np.asarray(x).astype(np.float64)


def striped(idx):
    return np.tile(np.asarray(idx).reshape(-1, 16).T, (8, 1)).astype(np.uint16)


def unstriped(offs):
    return offs[:16].T.reshape(-1).astype(np.int64)


E2M1 = np.array([0.0, 0.5, 1.0, 1.5, 2.0, 3.0, 4.0, 6.0, -0.0, -0.5, -1.0, -1.5, -2.0, -3.0, -4.0, -6.0])


def pack_weight(w, fmt):
    k, n = w.shape
    w = f64(np.asarray(w, np.float32).astype(ml_dtypes.bfloat16)).reshape(k // 32, 32, n)
    amax = np.abs(w).max(1)
    if fmt == "e4m3":
        byte = np.frexp(amax)[1] - 1 + 127 - 7
    else:
        mant, ex = np.frexp(amax / 6.0)
        byte = np.where(mant > 0.5, ex, ex - 1) + 127
    byte = np.clip(np.where(amax > 0, byte, 1), 1, 254)
    scaled = (w * np.exp2(127.0 - byte)[:, None, :]).reshape(k, n).astype(np.float32)
    by_word = np.ascontiguousarray(scaled.reshape(k // 512, 128, 4, n).transpose(0, 1, 3, 2))
    if fmt == "e4m3":
        words = by_word.astype(ml_dtypes.float8_e4m3fn).view(np.uint8)
    else:
        c = by_word.astype(ml_dtypes.float4_e2m1fn).view(np.uint8) & 0xF
        words = (c[..., 0::2] | (c[..., 1::2] << 4)).reshape(k // 512, 128, 2 * n)
    return np.ascontiguousarray(words), np.ascontiguousarray(byte.astype(np.uint8).reshape(k // 512, 16, n))


def unpack_weight(words, scales, fmt):
    g, _, n = scales.shape
    words = np.ascontiguousarray(words).reshape(g, 128, n, -1)
    if fmt == "e4m3":
        vals = words.view(ml_dtypes.float8_e4m3fn).astype(np.float64)
    else:
        nib = np.empty((g, 128, n, 4), np.uint8)
        nib[..., 0::2] = words & 0xF
        nib[..., 1::2] = words >> 4
        vals = E2M1[nib]
    vals = vals * np.repeat(np.exp2(scales.astype(np.float64) - 127.0), 8, axis=1)[..., None]
    return vals.transpose(0, 1, 3, 2).reshape(g * 512, n)


def sigmoid(v):
    return 1.0 / (1.0 + np.exp(-v))


D, E, T, I, Q, G = 512, 512, 2048, 512, 128, 64


def setup_inputs():
    n = np.random.standard_normal
    idx = np.random.permutation(T)[:I]
    fd = mx_kscale(D)
    fe = mx_kscale(E)
    keysp = pack_weight(n((D, T)) / fd[:, None], "e4m3")
    valsp = pack_weight(n((E, T)) / fe[:, None], "e4m3")
    return {
        "query": (n((D, Q)) * 0.8 / np.sqrt(D) * fd[:, None]).astype(np.float32),
        "keys_words": keysp[0],
        "keys_scales": keysp[1],
        "th": (np.random.uniform(1.8, 2.8, (Q, 1))).astype(np.float32),
        "gout": (n((E, Q)) * 1 / np.sqrt(E) * fe[:, None]).astype(np.float32),
        "vals_words": valsp[0],
        "vals_scales": valsp[1],
        "base": (0.5 * n((Q, I))).astype(np.float32),
        "offs": striped(idx),
    }


def reference(query, keys_words, keys_scales, th, gout, vals_words, vals_scales, base, offs):
    idx = unstriped(offs)
    keysu = unpack_weight(keys_words, keys_scales, "e4m3")
    valsu = unpack_weight(vals_words, vals_scales, "e4m3")
    queryq = mxq(f64(query), 0, "e4m3")
    keysidxg = keysu[:, idx]
    a = queryq.T @ keysidxg
    p = np.exp(a)
    s = p.reshape(Q, G, I // G).sum(axis=2)
    sh = sigmoid(np.log(s) - f64(th)) / s
    sr = np.repeat(sh, I // G, axis=1)
    goutq = mxq(f64(gout), 0, "e4m3")
    valsidxg = valsu[:, idx]
    c0 = goutq.T @ valsidxg
    dsr = c0 * p
    dsh = dsr.reshape(Q, G, I // G).sum(axis=2)
    ds = dsh / s * sigmoid(np.log(s) - f64(th)) * (1.0 - sigmoid(np.log(s) - f64(th))) / s - dsh * sigmoid(np.log(s) - f64(th)) / np.square(s)
    r1 = np.repeat(ds, I // G, axis=1)
    dp = c0 * sr + r1
    da = dp * p
    hda = da * 8.0 * 2.0 * 8.0
    hdp = hda * p
    hds = hdp.reshape(Q, G, I // G).sum(axis=2)
    hdsh = hds / s * (1.0 - sigmoid(np.log(s) - f64(th))) * sigmoid(np.log(s) - f64(th)) / s + hds * (-1.0) / np.square(s) * sigmoid(np.log(s) - f64(th))
    r51 = np.repeat(hdsh, I // G, axis=1)
    hsr = hdp * c0
    hsh = hsr.reshape(Q, G, I // G).sum(axis=2)
    hs = hds / s * (1.0 - sigmoid(np.log(s) - f64(th))) * dsh / s * sigmoid(np.log(s) - f64(th)) * (1.0 - sigmoid(np.log(s) - f64(th))) / s + hds / s * dsh / s * sigmoid(np.log(s) - f64(th)) * (-1.0) * sigmoid(np.log(s) - f64(th)) * (1.0 - sigmoid(np.log(s) - f64(th))) / s + hds * (-1.0) / np.square(s) * dsh * sigmoid(np.log(s) - f64(th)) * (1.0 - sigmoid(np.log(s) - f64(th))) / s + hds * (-1.0) * dsh * sigmoid(np.log(s) - f64(th)) / np.square(np.square(s)) * (-1.0) * s * 2.0 + hsh / s * sigmoid(np.log(s) - f64(th)) * (1.0 - sigmoid(np.log(s) - f64(th))) / s - hds / s * (1.0 - sigmoid(np.log(s) - f64(th))) * sigmoid(np.log(s) - f64(th)) * dsh / np.square(s) - hds * dsh / s * sigmoid(np.log(s) - f64(th)) * (1.0 - sigmoid(np.log(s) - f64(th))) / np.square(s) - hsh * sigmoid(np.log(s) - f64(th)) / np.square(s)
    r52 = np.repeat(hs, I // G, axis=1)
    hp = hda * dp + r51 * c0 + r52
    ha = hp * p
    y = ha + f64(base)
    return y

@@ -1,0 +1,165 @@
+import math
+from contextlib import ExitStack
+
+import concourse.mybir as mybir
+
+F32 = mybir.dt.float32
+BF16 = mybir.dt.bfloat16
+I32 = mybir.dt.int32
+U32 = mybir.dt.uint32
+U16 = mybir.dt.uint16
+U8 = mybir.dt.uint8
+FP8X4 = mybir.dt.float8_e4m3fn_x4
+ALU = mybir.AluOpType
+ACT = mybir.ActivationFunctionType
+AX = mybir.AxisListType
+
+P = 128
+PACK = 4
+TOKENS = 2048
+SLOTS = 512
+ROWS = 128
+GROUP = 8
+HALVES = 2
+HALF = SLOTS // HALVES
+HALF_GROUPS = HALF // GROUP
+VALS_PLANE = 4
+FLOPS = 2 * 2 * 512 * ROWS * SLOTS
+
+
+def tile_attend_gpgatedgroups_kernel(tc, query, keys_words, keys_scales, th, gout, vals_words, vals_scales, base, offs, out):
+    nc = tc.nc
+    with ExitStack() as ctx:
+        sb = ctx.enter_context(tc.tile_pool(name="sb", bufs=1))
+        ps = ctx.enter_context(tc.psum_pool(name="ps", bufs=1))
+
+        offsets = sb.tile([P, SLOTS // 16], U16, name="offsets")
+        key_pool = sb.tile([P, TOKENS], I32, name="key_pool", align_bytes=64)
+        val_pool = sb.tile([P, TOKENS], I32, name="val_pool", align_bytes=64)
+        key_scale_pool = sb.tile([P, TOKENS], U8, name="key_scale_pool", align_bytes=64)
+        val_scale_pool = sb.tile([P, TOKENS], U8, name="val_scale_pool", align_bytes=64)
+        query_raw = sb.tile([P, PACK, ROWS], F32, name="query_raw")
+        gout_raw = sb.tile([P, PACK, ROWS], F32, name="gout_raw")
+        th_col = sb.tile([P, 1], F32, name="th_col")
+        base_sb = sb.tile([P, SLOTS], F32, name="base_sb")
+
+        def load_scales(plane, scales, first):
+            for quad in range(4):
+                nc.sync.dma_start(
+                    out=plane[32 * quad + first : 32 * quad + first + 4, :].bitcast(I32),
+                    in_=scales[0, 4 * quad : 4 * quad + 4, :].bitcast(I32),
+                )
+
+        def load_words(pool_tile, words):
+            nc.sync.dma_start(out=pool_tile[:], in_=words[0].rearrange("p n t -> p (n t)").bitcast(I32))
+
+        nc.vector.memset(key_scale_pool[:].bitcast(I32), 0)
+        nc.gpsimd.memset(val_scale_pool[:].bitcast(I32), 0)
+        nc.sync.dma_start(offsets[:], offs)
+        nc.sync.dma_start(out=query_raw[:], in_=query.rearrange("(p j) q -> p j q", j=PACK))
+        load_scales(key_scale_pool, keys_scales, 0)
+        load_words(key_pool, keys_words)
+        nc.sync.dma_start(out=th_col[:], in_=th)
+        nc.sync.dma_start(out=gout_raw[:], in_=gout.rearrange("(p j) q -> p j q", j=PACK))
+        load_scales(val_scale_pool, vals_scales, VALS_PLANE)
+        load_words(val_pool, vals_words)
+        nc.sync.dma_start(out=base_sb[:], in_=base)
+
+        def quantise(raw, name):
+            grouped = sb.tile([P, ROWS, PACK], BF16, name=name + "_bf16", align_bytes=64)
+            codes = sb.tile([P, ROWS], U32, name=name + "_codes", align_bytes=64)
+            scales = sb.tile([P, ROWS], U8, name=name + "_scales", align_bytes=64)
+            nc.scalar.copy(out=grouped[:], in_=raw[:].rearrange("p j q -> p q j"))
+            nc.vector.quantize_mx(out=codes[:].bitcast(FP8X4), scales=scales[:], in_=grouped[:].rearrange("p q j -> p (q j)"))
+            return codes, scales
+
+        def gather_scales(plane, name):
+            picked = sb.tile([P, SLOTS], U8, name=name, align_bytes=64)
+            nc.vector.tensor_copy(out=picked[:], in_=plane[:].indirect(offsets[:]))
+            return picked
+
+        def product(pool_tile, picked_scales, first, codes, scales, half, name):
+            picked = sb.tile([P, HALF], U32, name=name + "_words", align_bytes=64)
+            cols = HALF // 16
+            nc.vector.tensor_copy(out=picked[:], in_=pool_tile[:].bitcast(U32).indirect(offsets[:, half * cols : (half + 1) * cols]))
+            acc = ps.tile([P, HALF], F32, name=name + "_acc")
+            nc.tensor.matmul_mx(
+                out=acc[:],
+                lhsT=codes[:].bitcast(FP8X4),
+                lhsT_scale=scales[:],
+                rhs=picked[:].bitcast(FP8X4),
+                rhs_scale=picked_scales[first:P, half * HALF : (half + 1) * HALF],
+                start=True,
+                stop=True,
+            )
+            return acc
+
+        def wide(name):
+            return [sb.tile([P, HALF], F32, name="%s%d" % (name, h)) for h in range(HALVES)]
+
+        def narrow(name):
+            return [sb.tile([P, HALF_GROUPS], F32, name="%s%d" % (name, h)) for h in range(HALVES)]
+
+        def by_group(t):
+            return t[:].rearrange("p (g j) -> p g j", j=GROUP)
+
+        def spread(t):
+            return t[:].unsqueeze(2).to_broadcast([P, HALF_GROUPS, GROUP])
+
+        halves = range(HALVES)
+
+        key_scales = gather_scales(key_scale_pool, "key_scales")
+        query_codes, query_scales = quantise(query_raw, "query")
+        score = [product(key_pool, key_scales, 0, query_codes, query_scales, h, "key%d" % h) for h in halves]
+
+        gate = sb.tile([P, 1], F32, name="gate")
+        nc.scalar.activation(out=gate[:], in_=th_col[:], func=ACT.Exp)
+        p = wide("p")
+        for h in halves:
+            nc.scalar.activation(out=p[h][:], in_=score[h][:], func=ACT.Exp)
+
+        val_scales = gather_scales(val_scale_pool, "val_scales")
+        gout_codes, gout_scales = quantise(gout_raw, "gout")
+
+        s, denom, inv = narrow("s"), narrow("denom"), narrow("inv")
+        v = wide("v")
+        for h in halves:
+            nc.vector.tensor_reduce(out=s[h][:], in_=by_group(p[h]), axis=AX.X, op=ALU.add)
+        c = [product(val_pool, val_scales, VALS_PLANE, gout_codes, gout_scales, h, "val%d" % h) for h in halves]
+
+        for h in halves:
+            nc.vector.tensor_scalar(out=denom[h][:], in0=s[h][:], scalar1=gate[:], scalar2=None, op0=ALU.add)
+        for h in halves:
+            nc.vector.reciprocal(out=inv[h][:], in_=denom[h][:])
+        for h in halves:
+            nc.vector.tensor_tensor(out=by_group(v[h]), in0=by_group(p[h]), in1=spread(inv[h]), op=ALU.mult)
+
+        vc, w, d, vd, dd = wide("vc"), wide("w"), wide("d"), wide("vd"), wide("dd")
+        mean, alpha, beta = narrow("mean"), narrow("alpha"), narrow("beta")
+        k, ad, bv, part, res = wide("k"), wide("ad"), wide("bv"), wide("part"), wide("res")
+        for h in halves:
+            nc.vector.tensor_tensor(out=vc[h][:], in0=c[h][:], in1=v[h][:], op=ALU.mult)
+        for h in halves:
+            nc.vector.tensor_reduce(out=mean[h][:], in_=by_group(vc[h]), axis=AX.X, op=ALU.add)
+        for h in halves:
+            nc.vector.tensor_tensor(out=by_group(w[h]), in0=by_group(c[h]), in1=spread(mean[h]), op=ALU.subtract)
+        for h in halves:
+            nc.vector.scalar_tensor_tensor(out=d[h][:], in0=w[h][:], scalar=math.sqrt(128.0), in1=v[h][:], op0=ALU.mult, op1=ALU.mult)
+        for h in halves:
+            nc.scalar.activation(out=dd[h][:], in_=d[h][:], func=ACT.Square)
+            nc.vector.tensor_tensor(out=vd[h][:], in0=d[h][:], in1=v[h][:], op=ALU.mult)
+        for h in halves:
+            nc.vector.tensor_reduce(out=alpha[h][:], in_=by_group(vd[h]), axis=AX.X, op=ALU.add)
+        for h in halves:
+            nc.vector.tensor_reduce(out=beta[h][:], in_=by_group(dd[h]), axis=AX.X, op=ALU.add)
+        for h in halves:
+            nc.vector.tensor_tensor(out=k[h][:], in0=dd[h][:], in1=base_sb[:, h * HALF : (h + 1) * HALF], op=ALU.add)
+        for h in halves:
+            nc.vector.tensor_tensor(out=by_group(ad[h]), in0=by_group(d[h]), in1=spread(alpha[h]), op=ALU.mult)
+        for h in halves:
+            nc.vector.tensor_tensor(out=by_group(bv[h]), in0=by_group(v[h]), in1=spread(beta[h]), op=ALU.mult)
+        for h in halves:
+            nc.vector.tensor_tensor(out=part[h][:], in0=k[h][:], in1=ad[h][:], op=ALU.subtract)
+        for h in halves:
+            nc.vector.tensor_tensor(out=res[h][:], in0=part[h][:], in1=bv[h][:], op=ALU.subtract)
+            nc.sync.dma_start(out=out[:, h * HALF : (h + 1) * HALF], in_=res[h][:])

@@ -24,81 +24,28 @@ HALVES = 2
 HALF = SLOTS // HALVES
 HALF_GROUPS = HALF // GROUP
 VALS_PLANE = 4
+POOL_COLS = 384
 FLOPS = 2 * 2 * 512 * ROWS * SLOTS
 
 
 def tile_attend_gpgatedgroups_kernel(tc, query, keys_words, keys_scales, th, gout, vals_words, vals_scales, base, offs, out):
     nc = tc.nc
+    halves = range(HALVES)
     with ExitStack() as ctx:
         sb = ctx.enter_context(tc.tile_pool(name="sb", bufs=1))
         ps = ctx.enter_context(tc.psum_pool(name="ps", bufs=1))
 
-        offsets = sb.tile([P, SLOTS // 16], U16, name="offsets")
-        key_pool = sb.tile([P, TOKENS], I32, name="key_pool", align_bytes=64)
-        val_pool = sb.tile([P, TOKENS], I32, name="val_pool", align_bytes=64)
-        key_scale_pool = sb.tile([P, TOKENS], U8, name="key_scale_pool", align_bytes=64)
-        val_scale_pool = sb.tile([P, TOKENS], U8, name="val_scale_pool", align_bytes=64)
-        query_raw = sb.tile([P, PACK, ROWS], F32, name="query_raw")
-        gout_raw = sb.tile([P, PACK, ROWS], F32, name="gout_raw")
-        th_col = sb.tile([P, 1], F32, name="th_col")
-        base_sb = sb.tile([P, SLOTS], F32, name="base_sb")
-
-        def load_scales(plane, scales, first):
-            for quad in range(4):
-                nc.sync.dma_start(
-                    out=plane[32 * quad + first : 32 * quad + first + 4, :].bitcast(I32),
-                    in_=scales[0, 4 * quad : 4 * quad + 4, :].bitcast(I32),
-                )
-
-        def load_words(pool_tile, words):
-            nc.sync.dma_start(out=pool_tile[:], in_=words[0].rearrange("p n t -> p (n t)").bitcast(I32))
-
-        nc.vector.memset(key_scale_pool[:].bitcast(I32), 0)
-        nc.gpsimd.memset(val_scale_pool[:].bitcast(I32), 0)
-        nc.sync.dma_start(offsets[:], offs)
-        nc.sync.dma_start(out=query_raw[:], in_=query.rearrange("(p j) q -> p j q", j=PACK))
-        load_scales(key_scale_pool, keys_scales, 0)
-        load_words(key_pool, keys_words)
-        nc.sync.dma_start(out=th_col[:], in_=th)
-        nc.sync.dma_start(out=gout_raw[:], in_=gout.rearrange("(p j) q -> p j q", j=PACK))
-        load_scales(val_scale_pool, vals_scales, VALS_PLANE)
-        load_words(val_pool, vals_words)
-        nc.sync.dma_start(out=base_sb[:], in_=base)
-
-        def quantise(raw, name):
-            grouped = sb.tile([P, ROWS, PACK], BF16, name=name + "_bf16", align_bytes=64)
-            codes = sb.tile([P, ROWS], U32, name=name + "_codes", align_bytes=64)
-            scales = sb.tile([P, ROWS], U8, name=name + "_scales", align_bytes=64)
-            nc.scalar.copy(out=grouped[:], in_=raw[:].rearrange("p j q -> p q j"))
-            nc.vector.quantize_mx(out=codes[:].bitcast(FP8X4), scales=scales[:], in_=grouped[:].rearrange("p q j -> p (q j)"))
-            return codes, scales
-
-        def gather_scales(plane, name):
-            picked = sb.tile([P, SLOTS], U8, name=name, align_bytes=64)
-            nc.vector.tensor_copy(out=picked[:], in_=plane[:].indirect(offsets[:]))
-            return picked
-
-        def product(pool_tile, picked_scales, first, codes, scales, half, name):
-            picked = sb.tile([P, HALF], U32, name=name + "_words", align_bytes=64)
-            cols = HALF // 16
-            nc.vector.tensor_copy(out=picked[:], in_=pool_tile[:].bitcast(U32).indirect(offsets[:, half * cols : (half + 1) * cols]))
-            acc = ps.tile([P, HALF], F32, name=name + "_acc")
-            nc.tensor.matmul_mx(
-                out=acc[:],
-                lhsT=codes[:].bitcast(FP8X4),
-                lhsT_scale=scales[:],
-                rhs=picked[:].bitcast(FP8X4),
-                rhs_scale=picked_scales[first:P, half * HALF : (half + 1) * HALF],
-                start=True,
-                stop=True,
-            )
-            return acc
+        def tile(name, shape, dtype, buffer=None):
+            return sb.tile(shape, dtype, name=name, tag=buffer or name, align_bytes=64)
 
         def wide(name):
-            return [sb.tile([P, HALF], F32, name="%s%d" % (name, h)) for h in range(HALVES)]
+            return [tile("%s%d" % (name, h), [P, HALF], F32) for h in halves]
 
         def narrow(name):
-            return [sb.tile([P, HALF_GROUPS], F32, name="%s%d" % (name, h)) for h in range(HALVES)]
+            return [tile("%s%d" % (name, h), [P, HALF_GROUPS], F32) for h in halves]
+
+        def half_of(t, h, width=HALF):
+            return t[:, h * width : (h + 1) * width]
 
         def by_group(t):
             return t[:].rearrange("p (g j) -> p g j", j=GROUP)
@@ -106,37 +53,117 @@ def tile_attend_gpgatedgroups_kernel(tc, query, keys_words, keys_scales, th, gou
         def spread(t):
             return t[:].unsqueeze(2).to_broadcast([P, HALF_GROUPS, GROUP])
 
-        halves = range(HALVES)
+        def load_scales(queue, plane, scales, first):
+            for quad in range(4):
+                queue.dma_start(
+                    out=plane[32 * quad + first : 32 * quad + first + 4, :].bitcast(I32),
+                    in_=scales[0, 4 * quad : 4 * quad + 4, :].bitcast(I32),
+                )
 
-        key_scales = gather_scales(key_scale_pool, "key_scales")
-        query_codes, query_scales = quantise(query_raw, "query")
-        score = [product(key_pool, key_scales, 0, query_codes, query_scales, h, "key%d" % h) for h in halves]
+        def load_words(pool_tile, words):
+            nc.sync.dma_start(out=pool_tile[:], in_=words[0].rearrange("p n t -> p (n t)").bitcast(I32))
 
-        gate = sb.tile([P, 1], F32, name="gate")
+        def load_rows(raw, rows):
+            nc.sync.dma_start(out=raw[:], in_=rows.rearrange("(p j) q -> p j q", j=PACK))
+
+        def round_rows(grouped, raw):
+            nc.scalar.copy(out=grouped[:], in_=raw[:].rearrange("p j q -> p q j"))
+
+        def quantise(codes, scales, grouped):
+            nc.vector.quantize_mx(out=codes[:].bitcast(FP8X4), scales=scales[:], in_=grouped[:].rearrange("p q j -> p (q j)"))
+
+        def gather_words(picked, pool_tile, h):
+            nc.vector.tensor_copy(out=picked, in_=pool_tile[:].bitcast(U32).indirect(half_of(offsets, h, HALF // 16)))
+
+        def product(name, codes, scales, picked, picked_scales):
+            acc = ps.tile([P, HALF], F32, name=name)
+            nc.tensor.matmul_mx(
+                out=acc[:],
+                lhsT=codes[:].bitcast(FP8X4),
+                lhsT_scale=scales[:],
+                rhs=picked.bitcast(FP8X4),
+                rhs_scale=picked_scales,
+                start=True,
+                stop=True,
+            )
+            return acc
+
+        offsets = tile("offsets", [P, SLOTS // 16], U16)
+        key_pool = tile("key_pool", [P, TOKENS], I32)
+        val_pool = tile("val_pool", [P, TOKENS], I32)
+        key_scale_pool = tile("key_scale_pool", [P, TOKENS], U8)
+        val_scale_pool = tile("val_scale_pool", [P, TOKENS], U8)
+        query_raw = tile("query_raw", [P, PACK, ROWS], F32)
+        th_col = tile("th_col", [P, 1], F32)
+
+        nc.vector.memset(key_scale_pool[:].bitcast(I32), 0)
+        nc.vector.memset(val_scale_pool[:].bitcast(I32), 0)
+        nc.sync.dma_start(offsets[:], offs)
+        load_words(key_pool, keys_words)
+        load_rows(query_raw, query)
+        load_words(val_pool, vals_words)
+        load_scales(nc.scalar, key_scale_pool, keys_scales, 0)
+        nc.gpsimd.dma_start(out=th_col[:], in_=th)
+        load_scales(nc.gpsimd, val_scale_pool, vals_scales, VALS_PLANE)
+
+        gate = tile("gate", [P, 1], F32)
         nc.scalar.activation(out=gate[:], in_=th_col[:], func=ACT.Exp)
+        query_bf16 = tile("query_bf16", [P, ROWS, PACK], BF16)
+        round_rows(query_bf16, query_raw)
+        gout_raw = tile("gout_raw", [P, PACK, ROWS], F32, "query_raw")
+        load_rows(gout_raw, gout)
+
+        key_scales = tile("key_scales", [P, SLOTS], U8)
+        nc.vector.tensor_copy(out=key_scales[:], in_=key_scale_pool[:].indirect(offsets[:]))
+        key_words = tile("key_words", [P, SLOTS], U32, "key_scale_pool")
+        for h in halves:
+            gather_words(half_of(key_words, h), key_pool, h)
+        query_codes = tile("query_codes", [P, ROWS], U32, "key_pool")
+        query_scales = tile("query_scales", [P, ROWS], U8)
+        quantise(query_codes, query_scales, query_bf16)
+        score = [product("score%d" % h, query_codes, query_scales, half_of(key_words, h), half_of(key_scales, h)) for h in halves]
+        base_sb = tile("base_sb", [P, SLOTS], F32, "key_pool")
+        nc.sync.dma_start(out=base_sb[:], in_=base)
+
         p = wide("p")
         for h in halves:
             nc.scalar.activation(out=p[h][:], in_=score[h][:], func=ACT.Exp)
+        gout_bf16 = tile("gout_bf16", [P, ROWS, PACK], BF16, "query_scales")
+        round_rows(gout_bf16, gout_raw)
 
-        val_scales = gather_scales(val_scale_pool, "val_scales")
-        gout_codes, gout_scales = quantise(gout_raw, "gout")
+        val_scales = tile("val_scales", [P, SLOTS], U8, "query_bf16")
+        nc.vector.tensor_copy(out=val_scales[:], in_=val_scale_pool[:].indirect(offsets[:]))
 
-        s, denom, inv = narrow("s"), narrow("denom"), narrow("inv")
-        v = wide("v")
+        s = tile("s", [P, SLOTS // GROUP], F32, "val_scale_pool")
+        denom, inv = narrow("denom"), narrow("inv")
+        v, vv = wide("v"), wide("vv")
         for h in halves:
-            nc.vector.tensor_reduce(out=s[h][:], in_=by_group(p[h]), axis=AX.X, op=ALU.add)
-        c = [product(val_pool, val_scales, VALS_PLANE, gout_codes, gout_scales, h, "val%d" % h) for h in halves]
-
+            nc.vector.tensor_reduce(out=half_of(s, h, HALF_GROUPS), in_=by_group(p[h]), axis=AX.X, op=ALU.add)
         for h in halves:
-            nc.vector.tensor_scalar(out=denom[h][:], in0=s[h][:], scalar1=gate[:], scalar2=None, op0=ALU.add)
+            nc.vector.tensor_scalar(out=denom[h][:], in0=half_of(s, h, HALF_GROUPS), scalar1=gate[:], scalar2=None, op0=ALU.add)
         for h in halves:
             nc.vector.reciprocal(out=inv[h][:], in_=denom[h][:])
         for h in halves:
-            nc.vector.tensor_tensor(out=by_group(v[h]), in0=by_group(p[h]), in1=spread(inv[h]), op=ALU.mult)
+            nc.gpsimd.tensor_tensor(out=by_group(v[h]), in0=by_group(p[h]), in1=spread(inv[h]), op=ALU.mult)
+        for h in halves:
+            nc.scalar.activation(out=vv[h][:], in_=v[h][:], func=ACT.Square, scale=128.0**0.25)
 
-        vc, w, d, vd, dd = wide("vc"), wide("w"), wide("d"), wide("vd"), wide("dd")
+        val_words = [tile("val_words0", [P, HALF], U32, "denom0")]
+        gather_words(val_words[0][:], val_pool, 0)
+        gout_codes = tile("gout_codes", [P, ROWS], U32, "denom1")
+        gout_scales = tile("gout_scales", [P, ROWS], U8)
+        quantise(gout_codes, gout_scales, gout_bf16)
+        val_words.append(tile("val_words1", [P, HALF], U32, "query_scales"))
+        gather_words(val_words[1][:], val_pool, 1)
+        c = [product("c%d" % h, gout_codes, gout_scales, val_words[h][:], half_of(val_scales, h)[VALS_PLANE:P, :]) for h in halves]
+
+        vc, d, vd = wide("vc"), wide("d"), wide("vd")
+        w_all = tile("w_all", [P, SLOTS], F32)
+        dd_all = tile("dd_all", [P, SLOTS], F32)
+        w = [half_of(w_all, h) for h in halves]
+        dd = [half_of(dd_all, h) for h in halves]
         mean, alpha, beta = narrow("mean"), narrow("alpha"), narrow("beta")
-        k, ad, bv, part, res = wide("k"), wide("ad"), wide("bv"), wide("part"), wide("res")
+        ad, bv, part, res = wide("ad"), wide("bv"), wide("part"), wide("res")
         for h in halves:
             nc.vector.tensor_tensor(out=vc[h][:], in0=c[h][:], in1=v[h][:], op=ALU.mult)
         for h in halves:
@@ -147,13 +174,15 @@ def tile_attend_gpgatedgroups_kernel(tc, query, keys_words, keys_scales, th, gou
             nc.vector.scalar_tensor_tensor(out=d[h][:], in0=w[h][:], scalar=math.sqrt(128.0), in1=v[h][:], op0=ALU.mult, op1=ALU.mult)
         for h in halves:
             nc.scalar.activation(out=dd[h][:], in_=d[h][:], func=ACT.Square)
-            nc.vector.tensor_tensor(out=vd[h][:], in0=d[h][:], in1=v[h][:], op=ALU.mult)
+            nc.vector.tensor_tensor(out=vd[h][:], in0=w[h][:], in1=vv[h][:], op=ALU.mult)
         for h in halves:
             nc.vector.tensor_reduce(out=alpha[h][:], in_=by_group(vd[h]), axis=AX.X, op=ALU.add)
         for h in halves:
             nc.vector.tensor_reduce(out=beta[h][:], in_=by_group(dd[h]), axis=AX.X, op=ALU.add)
-        for h in halves:
-            nc.vector.tensor_tensor(out=k[h][:], in0=dd[h][:], in1=base_sb[:, h * HALF : (h + 1) * HALF], op=ALU.add)
+        k_all = tile("k_all", [P, SLOTS], F32, "w_all")
+        k = [half_of(k_all, h) for h in halves]
+        nc.gpsimd.tensor_tensor(out=k_all[:, :POOL_COLS], in0=dd_all[:, :POOL_COLS], in1=base_sb[:, :POOL_COLS], op=ALU.add)
+        nc.vector.tensor_tensor(out=k_all[:, POOL_COLS:], in0=dd_all[:, POOL_COLS:], in1=base_sb[:, POOL_COLS:], op=ALU.add)
         for h in halves:
             nc.vector.tensor_tensor(out=by_group(ad[h]), in0=by_group(d[h]), in1=spread(alpha[h]), op=ALU.mult)
         for h in halves:
@@ -162,4 +191,4 @@ def tile_attend_gpgatedgroups_kernel(tc, query, keys_words, keys_scales, th, gou
             nc.vector.tensor_tensor(out=part[h][:], in0=k[h][:], in1=ad[h][:], op=ALU.subtract)
         for h in halves:
             nc.vector.tensor_tensor(out=res[h][:], in0=part[h][:], in1=bv[h][:], op=ALU.subtract)
-            nc.sync.dma_start(out=out[:, h * HALF : (h + 1) * HALF], in_=res[h][:])
+            nc.sync.dma_start(out=half_of(out, h), in_=res[h][:])

@@ -25,6 +25,7 @@ HALF = SLOTS // HALVES
 HALF_GROUPS = HALF // GROUP
 VALS_PLANE = 4
 POOL_COLS = 384
+PITCH = 12
 FLOPS = 2 * 2 * 512 * ROWS * SLOTS
 
 
@@ -53,9 +54,9 @@ def tile_attend_gpgatedgroups_kernel(tc, query, keys_words, keys_scales, th, gou
         def spread(t):
             return t[:].unsqueeze(2).to_broadcast([P, HALF_GROUPS, GROUP])
 
-        def load_scales(queue, plane, scales, first):
+        def load_scales(queues, plane, scales, first):
             for quad in range(4):
-                queue.dma_start(
+                queues[quad].dma_start(
                     out=plane[32 * quad + first : 32 * quad + first + 4, :].bitcast(I32),
                     in_=scales[0, 4 * quad : 4 * quad + 4, :].bitcast(I32),
                 )
@@ -96,65 +97,66 @@ def tile_attend_gpgatedgroups_kernel(tc, query, keys_words, keys_scales, th, gou
         query_raw = tile("query_raw", [P, PACK, ROWS], F32)
         th_col = tile("th_col", [P, 1], F32)
 
-        nc.vector.memset(key_scale_pool[:].bitcast(I32), 0)
-        nc.vector.memset(val_scale_pool[:].bitcast(I32), 0)
-        nc.sync.dma_start(offsets[:], offs)
-        load_words(key_pool, keys_words)
-        load_rows(query_raw, query)
-        load_words(val_pool, vals_words)
-        load_scales(nc.scalar, key_scale_pool, keys_scales, 0)
-        nc.gpsimd.dma_start(out=th_col[:], in_=th)
-        load_scales(nc.gpsimd, val_scale_pool, vals_scales, VALS_PLANE)
+        gout_raw = tile("gout_raw", [P, PACK, ROWS], F32)
+        base_sb = tile("base_sb", [P, SLOTS], F32)
 
-        gate = tile("gate", [P, 1], F32)
-        nc.scalar.activation(out=gate[:], in_=th_col[:], func=ACT.Exp)
+        nc.vector.memset(key_scale_pool[:].bitcast(I32), 0)
+        nc.gpsimd.memset(val_scale_pool[:].bitcast(I32), 0)
+        nc.sync.dma_start(offsets[:], offs)
+        nc.scalar.dma_start(out=th_col[:], in_=th)
+        load_rows(query_raw, query)
+        load_scales([nc.sync, nc.scalar] * 2, key_scale_pool, keys_scales, 0)
+        load_words(key_pool, keys_words)
+        load_scales([nc.sync] * 4, val_scale_pool, vals_scales, VALS_PLANE)
+        load_rows(gout_raw, gout)
+        load_words(val_pool, vals_words)
+        nc.sync.dma_start(out=base_sb[:], in_=base)
+
+        p = [tile("p%d" % h, [P, HALF_GROUPS, PITCH], F32) for h in halves]
+        for h in halves:
+            nc.scalar.activation(out=p[h][:, :, GROUP], in_=th_col[:].to_broadcast([P, HALF_GROUPS]), func=ACT.Exp)
         query_bf16 = tile("query_bf16", [P, ROWS, PACK], BF16)
         round_rows(query_bf16, query_raw)
-        gout_raw = tile("gout_raw", [P, PACK, ROWS], F32, "query_raw")
-        load_rows(gout_raw, gout)
 
         key_scales = tile("key_scales", [P, SLOTS], U8)
         nc.vector.tensor_copy(out=key_scales[:], in_=key_scale_pool[:].indirect(offsets[:]))
-        key_words = tile("key_words", [P, SLOTS], U32, "key_scale_pool")
-        for h in halves:
-            gather_words(half_of(key_words, h), key_pool, h)
-        query_codes = tile("query_codes", [P, ROWS], U32, "key_pool")
+        key_words = tile("key_words", [P, SLOTS], U32)
+        query_codes = tile("query_codes", [P, ROWS], U32)
         query_scales = tile("query_scales", [P, ROWS], U8)
         quantise(query_codes, query_scales, query_bf16)
-        score = [product("score%d" % h, query_codes, query_scales, half_of(key_words, h), half_of(key_scales, h)) for h in halves]
-        base_sb = tile("base_sb", [P, SLOTS], F32, "key_pool")
-        nc.sync.dma_start(out=base_sb[:], in_=base)
-
-        p = wide("p")
         for h in halves:
-            nc.scalar.activation(out=p[h][:], in_=score[h][:], func=ACT.Exp)
-        gout_bf16 = tile("gout_bf16", [P, ROWS, PACK], BF16, "query_scales")
+            gather_words(half_of(key_words, h), key_pool, h)
+        score = [product("score%d" % h, query_codes, query_scales, half_of(key_words, h), half_of(key_scales, h)) for h in halves]
+
+        for h in halves:
+            nc.scalar.activation(out=p[h][:, :, :GROUP], in_=by_group(score[h]), func=ACT.Exp)
+        gout_bf16 = tile("gout_bf16", [P, ROWS, PACK], BF16)
         round_rows(gout_bf16, gout_raw)
 
-        val_scales = tile("val_scales", [P, SLOTS], U8, "query_bf16")
+        val_scales = tile("val_scales", [P, SLOTS], U8)
         nc.vector.tensor_copy(out=val_scales[:], in_=val_scale_pool[:].indirect(offsets[:]))
 
-        s = tile("s", [P, SLOTS // GROUP], F32, "val_scale_pool")
-        denom, inv = narrow("denom"), narrow("inv")
-        v, vv = wide("v"), wide("vv")
+        denom_all = tile("denom_all", [P, SLOTS // GROUP], F32, "val_scale_pool")
+        denom = [half_of(denom_all, h, HALF_GROUPS) for h in halves]
+        inv = narrow("inv")
+        v = wide("v")
+        vv_all = tile("vv_all", [P, SLOTS], F32, "gout_raw")
+        vv = [half_of(vv_all, h) for h in halves]
         for h in halves:
-            nc.vector.tensor_reduce(out=half_of(s, h, HALF_GROUPS), in_=by_group(p[h]), axis=AX.X, op=ALU.add)
-        for h in halves:
-            nc.vector.tensor_scalar(out=denom[h][:], in0=half_of(s, h, HALF_GROUPS), scalar1=gate[:], scalar2=None, op0=ALU.add)
+            nc.vector.tensor_reduce(out=denom[h][:], in_=p[h][:, :, : GROUP + 1], axis=AX.X, op=ALU.add)
         for h in halves:
             nc.vector.reciprocal(out=inv[h][:], in_=denom[h][:])
         for h in halves:
-            nc.gpsimd.tensor_tensor(out=by_group(v[h]), in0=by_group(p[h]), in1=spread(inv[h]), op=ALU.mult)
+            nc.gpsimd.tensor_tensor(out=by_group(v[h]), in0=p[h][:, :, :GROUP], in1=spread(inv[h]), op=ALU.mult)
         for h in halves:
             nc.scalar.activation(out=vv[h][:], in_=v[h][:], func=ACT.Square, scale=128.0**0.25)
 
-        val_words = [tile("val_words0", [P, HALF], U32, "denom0")]
-        gather_words(val_words[0][:], val_pool, 0)
-        gout_codes = tile("gout_codes", [P, ROWS], U32, "denom1")
+        gout_codes = tile("gout_codes", [P, ROWS], U32)
         gout_scales = tile("gout_scales", [P, ROWS], U8)
         quantise(gout_codes, gout_scales, gout_bf16)
-        val_words.append(tile("val_words1", [P, HALF], U32, "query_scales"))
-        gather_words(val_words[1][:], val_pool, 1)
+        val_words = [tile("val_words%d" % h, [P, HALF], U32) for h in halves]
+        for h in halves:
+            gather_words(val_words[h][:], val_pool, h)
         c = [product("c%d" % h, gout_codes, gout_scales, val_words[h][:], half_of(val_scales, h)[VALS_PLANE:P, :]) for h in halves]
 
         vc, d, vd = wide("vc"), wide("d"), wide("vd")

@@ -24,7 +24,6 @@ HALVES = 2
 HALF = SLOTS // HALVES
 HALF_GROUPS = HALF // GROUP
 VALS_PLANE = 4
-POOL_COLS = 384
 PITCH = 12
 FLOPS = 2 * 2 * 512 * ROWS * SLOTS
 
@@ -55,10 +54,10 @@ def tile_attend_gpgatedgroups_kernel(tc, query, keys_words, keys_scales, th, gou
             return t[:].unsqueeze(2).to_broadcast([P, HALF_GROUPS, GROUP])
 
         def load_scales(queues, plane, scales, first):
-            for quad in range(4):
-                queues[quad].dma_start(
-                    out=plane[32 * quad + first : 32 * quad + first + 4, :].bitcast(I32),
-                    in_=scales[0, 4 * quad : 4 * quad + 4, :].bitcast(I32),
+            for row in range(4):
+                queues[row].dma_start(
+                    out=plane[first + row : P : 32, :].bitcast(I32),
+                    in_=scales[0, row:16:4, :].bitcast(I32),
                 )
 
         def load_words(pool_tile, words):
@@ -101,7 +100,7 @@ def tile_attend_gpgatedgroups_kernel(tc, query, keys_words, keys_scales, th, gou
         base_sb = tile("base_sb", [P, SLOTS], F32)
 
         nc.vector.memset(key_scale_pool[:].bitcast(I32), 0)
-        nc.gpsimd.memset(val_scale_pool[:].bitcast(I32), 0)
+        nc.vector.memset(val_scale_pool[:].bitcast(I32), 0)
         nc.sync.dma_start(offsets[:], offs)
         nc.scalar.dma_start(out=th_col[:], in_=th)
         load_rows(query_raw, query)
@@ -139,17 +138,11 @@ def tile_attend_gpgatedgroups_kernel(tc, query, keys_words, keys_scales, th, gou
         denom_all = tile("denom_all", [P, SLOTS // GROUP], F32, "val_scale_pool")
         denom = [half_of(denom_all, h, HALF_GROUPS) for h in halves]
         inv = narrow("inv")
-        v = wide("v")
-        vv_all = tile("vv_all", [P, SLOTS], F32, "gout_raw")
-        vv = [half_of(vv_all, h) for h in halves]
+
         for h in halves:
             nc.vector.tensor_reduce(out=denom[h][:], in_=p[h][:, :, : GROUP + 1], axis=AX.X, op=ALU.add)
         for h in halves:
             nc.vector.reciprocal(out=inv[h][:], in_=denom[h][:])
-        for h in halves:
-            nc.gpsimd.tensor_tensor(out=by_group(v[h]), in0=p[h][:, :, :GROUP], in1=spread(inv[h]), op=ALU.mult)
-        for h in halves:
-            nc.scalar.activation(out=vv[h][:], in_=v[h][:], func=ACT.Square, scale=128.0**0.25)
 
         gout_codes = tile("gout_codes", [P, ROWS], U32)
         gout_scales = tile("gout_scales", [P, ROWS], U8)
@@ -159,11 +152,13 @@ def tile_attend_gpgatedgroups_kernel(tc, query, keys_words, keys_scales, th, gou
             gather_words(val_words[h][:], val_pool, h)
         c = [product("c%d" % h, gout_codes, gout_scales, val_words[h][:], half_of(val_scales, h)[VALS_PLANE:P, :]) for h in halves]
 
+        v_all = tile("v_all", [P, SLOTS], F32, "val_pool")
+        v = [half_of(v_all, h) for h in halves]
+        for h in halves:
+            nc.vector.tensor_tensor(out=by_group(v[h]), in0=p[h][:, :, :GROUP], in1=spread(inv[h]), op=ALU.mult)
+
         vc, d, vd = wide("vc"), wide("d"), wide("vd")
-        w_all = tile("w_all", [P, SLOTS], F32)
-        dd_all = tile("dd_all", [P, SLOTS], F32)
-        w = [half_of(w_all, h) for h in halves]
-        dd = [half_of(dd_all, h) for h in halves]
+        w, dd, k = wide("w"), wide("dd"), wide("k")
         mean, alpha, beta = narrow("mean"), narrow("alpha"), narrow("beta")
         ad, bv, part, res = wide("ad"), wide("bv"), wide("part"), wide("res")
         for h in halves:
@@ -176,15 +171,13 @@ def tile_attend_gpgatedgroups_kernel(tc, query, keys_words, keys_scales, th, gou
             nc.vector.scalar_tensor_tensor(out=d[h][:], in0=w[h][:], scalar=math.sqrt(128.0), in1=v[h][:], op0=ALU.mult, op1=ALU.mult)
         for h in halves:
             nc.scalar.activation(out=dd[h][:], in_=d[h][:], func=ACT.Square)
-            nc.vector.tensor_tensor(out=vd[h][:], in0=w[h][:], in1=vv[h][:], op=ALU.mult)
+            nc.vector.tensor_tensor(out=vd[h][:], in0=d[h][:], in1=v[h][:], op=ALU.mult)
         for h in halves:
             nc.vector.tensor_reduce(out=alpha[h][:], in_=by_group(vd[h]), axis=AX.X, op=ALU.add)
         for h in halves:
             nc.vector.tensor_reduce(out=beta[h][:], in_=by_group(dd[h]), axis=AX.X, op=ALU.add)
-        k_all = tile("k_all", [P, SLOTS], F32, "w_all")
-        k = [half_of(k_all, h) for h in halves]
-        nc.gpsimd.tensor_tensor(out=k_all[:, :POOL_COLS], in0=dd_all[:, :POOL_COLS], in1=base_sb[:, :POOL_COLS], op=ALU.add)
-        nc.vector.tensor_tensor(out=k_all[:, POOL_COLS:], in0=dd_all[:, POOL_COLS:], in1=base_sb[:, POOL_COLS:], op=ALU.add)
+        for h in halves:
+            nc.vector.tensor_tensor(out=k[h][:], in0=dd[h][:], in1=half_of(base_sb, h), op=ALU.add)
         for h in halves:
             nc.vector.tensor_tensor(out=by_group(ad[h]), in0=by_group(d[h]), in1=spread(alpha[h]), op=ALU.mult)
         for h in halves:

@@ -16,16 +16,21 @@ AX = mybir.AxisListType
 
 P = 128
 PACK = 4
+FEATURES = P * PACK
 TOKENS = 2048
 SLOTS = 512
 ROWS = 128
 GROUP = 8
+LIST_ROWS = 16
+QUADRANT = 32
+SCALE_ROWS = 4
 HALVES = 2
 HALF = SLOTS // HALVES
 HALF_GROUPS = HALF // GROUP
-VALS_PLANE = 4
+VAL_SCALE_FIRST = 4
 PITCH = 12
-FLOPS = 2 * 2 * 512 * ROWS * SLOTS
+PENALTY = 8.0 * 2.0 * 8.0
+FLOPS = 2 * 2 * FEATURES * ROWS * SLOTS
 
 
 def tile_attend_gpgatedgroups_kernel(tc, query, keys_words, keys_scales, th, gout, vals_words, vals_scales, base, offs, out):
@@ -38,10 +43,10 @@ def tile_attend_gpgatedgroups_kernel(tc, query, keys_words, keys_scales, th, gou
         def tile(name, shape, dtype, buffer=None):
             return sb.tile(shape, dtype, name=name, tag=buffer or name, align_bytes=64)
 
-        def wide(name):
+        def per_slot(name):
             return [tile("%s%d" % (name, h), [P, HALF], F32) for h in halves]
 
-        def narrow(name):
+        def per_group(name):
             return [tile("%s%d" % (name, h), [P, HALF_GROUPS], F32) for h in halves]
 
         def half_of(t, h, width=HALF):
@@ -53,15 +58,15 @@ def tile_attend_gpgatedgroups_kernel(tc, query, keys_words, keys_scales, th, gou
         def spread(t):
             return t[:].unsqueeze(2).to_broadcast([P, HALF_GROUPS, GROUP])
 
-        def load_scales(queues, plane, scales, first):
-            for row in range(4):
-                queues[row].dma_start(
-                    out=plane[first + row : P : 32, :].bitcast(I32),
-                    in_=scales[0, row:16:4, :].bitcast(I32),
+        def load_scales(scale_pool, scales, first):
+            for r in range(SCALE_ROWS):
+                nc.sync.dma_start(
+                    out=scale_pool[first + r : P : QUADRANT, :].bitcast(I32),
+                    in_=scales[0, r : FEATURES // QUADRANT : SCALE_ROWS, :].bitcast(I32),
                 )
 
-        def load_words(pool_tile, words):
-            nc.sync.dma_start(out=pool_tile[:], in_=words[0].rearrange("p n t -> p (n t)").bitcast(I32))
+        def load_words(word_pool, words):
+            nc.sync.dma_start(out=word_pool[:], in_=words[0].rearrange("p n t -> p (n t)").bitcast(I32))
 
         def load_rows(raw, rows):
             nc.sync.dma_start(out=raw[:], in_=rows.rearrange("(p j) q -> p j q", j=PACK))
@@ -72,8 +77,8 @@ def tile_attend_gpgatedgroups_kernel(tc, query, keys_words, keys_scales, th, gou
         def quantise(codes, scales, grouped):
             nc.vector.quantize_mx(out=codes[:].bitcast(FP8X4), scales=scales[:], in_=grouped[:].rearrange("p q j -> p (q j)"))
 
-        def gather_words(picked, pool_tile, h):
-            nc.vector.tensor_copy(out=picked, in_=pool_tile[:].bitcast(U32).indirect(half_of(offsets, h, HALF // 16)))
+        def gather_words(picked, word_pool, h):
+            nc.vector.tensor_copy(out=picked, in_=word_pool[:].bitcast(U32).indirect(half_of(offsets, h, HALF // LIST_ROWS)))
 
         def product(name, codes, scales, picked, picked_scales):
             acc = ps.tile([P, HALF], F32, name=name)
@@ -88,32 +93,32 @@ def tile_attend_gpgatedgroups_kernel(tc, query, keys_words, keys_scales, th, gou
             )
             return acc
 
-        offsets = tile("offsets", [P, SLOTS // 16], U16)
+        offsets = tile("offsets", [P, SLOTS // LIST_ROWS], U16)
         key_pool = tile("key_pool", [P, TOKENS], I32)
         val_pool = tile("val_pool", [P, TOKENS], I32)
         key_scale_pool = tile("key_scale_pool", [P, TOKENS], U8)
         val_scale_pool = tile("val_scale_pool", [P, TOKENS], U8)
         query_raw = tile("query_raw", [P, PACK, ROWS], F32)
         th_col = tile("th_col", [P, 1], F32)
-
         gout_raw = tile("gout_raw", [P, PACK, ROWS], F32)
         base_sb = tile("base_sb", [P, SLOTS], F32)
 
         nc.vector.memset(key_scale_pool[:].bitcast(I32), 0)
         nc.vector.memset(val_scale_pool[:].bitcast(I32), 0)
+
         nc.sync.dma_start(offsets[:], offs)
-        nc.scalar.dma_start(out=th_col[:], in_=th)
         load_rows(query_raw, query)
-        load_scales([nc.sync, nc.scalar] * 2, key_scale_pool, keys_scales, 0)
+        load_scales(key_scale_pool, keys_scales, 0)
         load_words(key_pool, keys_words)
-        load_scales([nc.sync] * 4, val_scale_pool, vals_scales, VALS_PLANE)
+        nc.sync.dma_start(out=th_col[:], in_=th)
+        load_scales(val_scale_pool, vals_scales, VAL_SCALE_FIRST)
         load_rows(gout_raw, gout)
         load_words(val_pool, vals_words)
         nc.sync.dma_start(out=base_sb[:], in_=base)
 
-        p = [tile("p%d" % h, [P, HALF_GROUPS, PITCH], F32) for h in halves]
+        expo = [tile("expo%d" % h, [P, HALF_GROUPS, PITCH], F32) for h in halves]
         for h in halves:
-            nc.scalar.activation(out=p[h][:, :, GROUP], in_=th_col[:].to_broadcast([P, HALF_GROUPS]), func=ACT.Exp)
+            nc.scalar.activation(out=expo[h][:, :, GROUP], in_=th_col[:].to_broadcast([P, HALF_GROUPS]), func=ACT.Exp)
         query_bf16 = tile("query_bf16", [P, ROWS, PACK], BF16)
         round_rows(query_bf16, query_raw)
 
@@ -128,7 +133,7 @@ def tile_attend_gpgatedgroups_kernel(tc, query, keys_words, keys_scales, th, gou
         score = [product("score%d" % h, query_codes, query_scales, half_of(key_words, h), half_of(key_scales, h)) for h in halves]
 
         for h in halves:
-            nc.scalar.activation(out=p[h][:, :, :GROUP], in_=by_group(score[h]), func=ACT.Exp)
+            nc.scalar.activation(out=expo[h][:, :, :GROUP], in_=by_group(score[h]), func=ACT.Exp)
         gout_bf16 = tile("gout_bf16", [P, ROWS, PACK], BF16)
         round_rows(gout_bf16, gout_raw)
 
@@ -137,12 +142,14 @@ def tile_attend_gpgatedgroups_kernel(tc, query, keys_words, keys_scales, th, gou
 
         denom_all = tile("denom_all", [P, SLOTS // GROUP], F32, "val_scale_pool")
         denom = [half_of(denom_all, h, HALF_GROUPS) for h in halves]
-        inv = narrow("inv")
-
+        inv = per_group("inv")
         for h in halves:
-            nc.vector.tensor_reduce(out=denom[h][:], in_=p[h][:, :, : GROUP + 1], axis=AX.X, op=ALU.add)
+            nc.vector.tensor_reduce(out=denom[h][:], in_=expo[h][:, :, : GROUP + 1], axis=AX.X, op=ALU.add)
         for h in halves:
             nc.vector.reciprocal(out=inv[h][:], in_=denom[h][:])
+
+        share = [tile("share0", [P, HALF], F32)]
+        nc.vector.tensor_tensor(out=by_group(share[0]), in0=expo[0][:, :, :GROUP], in1=spread(inv[0]), op=ALU.mult)
 
         gout_codes = tile("gout_codes", [P, ROWS], U32)
         gout_scales = tile("gout_scales", [P, ROWS], U8)
@@ -150,40 +157,43 @@ def tile_attend_gpgatedgroups_kernel(tc, query, keys_words, keys_scales, th, gou
         val_words = [tile("val_words%d" % h, [P, HALF], U32) for h in halves]
         for h in halves:
             gather_words(val_words[h][:], val_pool, h)
-        c = [product("c%d" % h, gout_codes, gout_scales, val_words[h][:], half_of(val_scales, h)[VALS_PLANE:P, :]) for h in halves]
+        c = [product("c%d" % h, gout_codes, gout_scales, val_words[h][:], half_of(val_scales, h)[VAL_SCALE_FIRST:P, :]) for h in halves]
 
-        v_all = tile("v_all", [P, SLOTS], F32, "val_pool")
-        v = [half_of(v_all, h) for h in halves]
-        for h in halves:
-            nc.vector.tensor_tensor(out=by_group(v[h]), in0=p[h][:, :, :GROUP], in1=spread(inv[h]), op=ALU.mult)
+        share.append(tile("share1", [P, HALF], F32, "val_pool"))
+        nc.vector.tensor_tensor(out=by_group(share[1]), in0=expo[1][:, :, :GROUP], in1=spread(inv[1]), op=ALU.mult)
 
-        vc, d, vd = wide("vc"), wide("d"), wide("vd")
-        w, dd, k = wide("w"), wide("dd"), wide("k")
-        mean, alpha, beta = narrow("mean"), narrow("alpha"), narrow("beta")
-        ad, bv, part, res = wide("ad"), wide("bv"), wide("part"), wide("res")
+        share_c, grad, share_grad = per_slot("share_c"), per_slot("grad"), per_slot("share_grad")
+        centred, grad_sq, with_base = per_slot("centred"), per_slot("grad_sq"), per_slot("with_base")
+        sum_share_c, sum_share_grad, sum_grad_sq = per_group("sum_share_c"), per_group("sum_share_grad"), per_group("sum_grad_sq")
+        grad_term, share_term, partial, result = per_slot("grad_term"), per_slot("share_term"), per_slot("partial"), per_slot("result")
+
         for h in halves:
-            nc.vector.tensor_tensor(out=vc[h][:], in0=c[h][:], in1=v[h][:], op=ALU.mult)
+            nc.vector.tensor_tensor(out=share_c[h][:], in0=c[h][:], in1=share[h][:], op=ALU.mult)
         for h in halves:
-            nc.vector.tensor_reduce(out=mean[h][:], in_=by_group(vc[h]), axis=AX.X, op=ALU.add)
+            nc.vector.tensor_reduce(out=sum_share_c[h][:], in_=by_group(share_c[h]), axis=AX.X, op=ALU.add)
         for h in halves:
-            nc.vector.tensor_tensor(out=by_group(w[h]), in0=by_group(c[h]), in1=spread(mean[h]), op=ALU.subtract)
+            nc.vector.tensor_tensor(out=by_group(centred[h]), in0=by_group(c[h]), in1=spread(sum_share_c[h]), op=ALU.subtract)
         for h in halves:
-            nc.vector.scalar_tensor_tensor(out=d[h][:], in0=w[h][:], scalar=math.sqrt(128.0), in1=v[h][:], op0=ALU.mult, op1=ALU.mult)
+            nc.vector.scalar_tensor_tensor(
+                out=grad[h][:], in0=centred[h][:], scalar=math.sqrt(PENALTY), in1=share[h][:], op0=ALU.mult, op1=ALU.mult
+            )
+
         for h in halves:
-            nc.scalar.activation(out=dd[h][:], in_=d[h][:], func=ACT.Square)
-            nc.vector.tensor_tensor(out=vd[h][:], in0=d[h][:], in1=v[h][:], op=ALU.mult)
+            nc.scalar.activation(out=grad_sq[h][:], in_=grad[h][:], func=ACT.Square)
+            nc.vector.tensor_tensor(out=share_grad[h][:], in0=grad[h][:], in1=share[h][:], op=ALU.mult)
         for h in halves:
-            nc.vector.tensor_reduce(out=alpha[h][:], in_=by_group(vd[h]), axis=AX.X, op=ALU.add)
+            nc.vector.tensor_reduce(out=sum_share_grad[h][:], in_=by_group(share_grad[h]), axis=AX.X, op=ALU.add)
         for h in halves:
-            nc.vector.tensor_reduce(out=beta[h][:], in_=by_group(dd[h]), axis=AX.X, op=ALU.add)
+            nc.vector.tensor_reduce(out=sum_grad_sq[h][:], in_=by_group(grad_sq[h]), axis=AX.X, op=ALU.add)
+
         for h in halves:
-            nc.vector.tensor_tensor(out=k[h][:], in0=dd[h][:], in1=half_of(base_sb, h), op=ALU.add)
+            nc.vector.tensor_tensor(out=with_base[h][:], in0=grad_sq[h][:], in1=half_of(base_sb, h), op=ALU.add)
         for h in halves:
-            nc.vector.tensor_tensor(out=by_group(ad[h]), in0=by_group(d[h]), in1=spread(alpha[h]), op=ALU.mult)
+            nc.vector.tensor_tensor(out=by_group(grad_term[h]), in0=by_group(grad[h]), in1=spread(sum_share_grad[h]), op=ALU.mult)
         for h in halves:
-            nc.vector.tensor_tensor(out=by_group(bv[h]), in0=by_group(v[h]), in1=spread(beta[h]), op=ALU.mult)
+            nc.vector.tensor_tensor(out=by_group(share_term[h]), in0=by_group(share[h]), in1=spread(sum_grad_sq[h]), op=ALU.mult)
         for h in halves:
-            nc.vector.tensor_tensor(out=part[h][:], in0=k[h][:], in1=ad[h][:], op=ALU.subtract)
+            nc.vector.tensor_tensor(out=partial[h][:], in0=with_base[h][:], in1=grad_term[h][:], op=ALU.subtract)
         for h in halves:
-            nc.vector.tensor_tensor(out=res[h][:], in0=part[h][:], in1=bv[h][:], op=ALU.subtract)
-            nc.sync.dma_start(out=half_of(out, h), in_=res[h][:])
+            nc.vector.tensor_tensor(out=result[h][:], in0=partial[h][:], in1=share_term[h][:], op=ALU.subtract)
+            nc.sync.dma_start(out=half_of(out, h), in_=result[h][:])

import math
from contextlib import ExitStack

import concourse.mybir as mybir

F32 = mybir.dt.float32
BF16 = mybir.dt.bfloat16
I32 = mybir.dt.int32
U32 = mybir.dt.uint32
U16 = mybir.dt.uint16
U8 = mybir.dt.uint8
FP8X4 = mybir.dt.float8_e4m3fn_x4
ALU = mybir.AluOpType
ACT = mybir.ActivationFunctionType
AX = mybir.AxisListType

P = 128
PACK = 4
FEATURES = P * PACK
TOKENS = 2048
SLOTS = 512
ROWS = 128
GROUP = 8
LIST_ROWS = 16
QUADRANT = 32
SCALE_ROWS = 4
HALVES = 2
HALF = SLOTS // HALVES
HALF_GROUPS = HALF // GROUP
VAL_SCALE_FIRST = 4
PITCH = 12
PENALTY = 8.0 * 2.0 * 8.0
FLOPS = 2 * 2 * FEATURES * ROWS * SLOTS


def tile_attend_gpgatedgroups_kernel(tc, query, keys_words, keys_scales, th, gout, vals_words, vals_scales, base, offs, out):
    nc = tc.nc
    halves = range(HALVES)
    with ExitStack() as ctx:
        sb = ctx.enter_context(tc.tile_pool(name="sb", bufs=1))
        ps = ctx.enter_context(tc.psum_pool(name="ps", bufs=1))

        def tile(name, shape, dtype, buffer=None):
            return sb.tile(shape, dtype, name=name, tag=buffer or name, align_bytes=64)

        def per_slot(name):
            return [tile("%s%d" % (name, h), [P, HALF], F32) for h in halves]

        def per_group(name):
            return [tile("%s%d" % (name, h), [P, HALF_GROUPS], F32) for h in halves]

        def half_of(t, h, width=HALF):
            return t[:, h * width : (h + 1) * width]

        def by_group(t):
            return t[:].rearrange("p (g j) -> p g j", j=GROUP)

        def spread(t):
            return t[:].unsqueeze(2).to_broadcast([P, HALF_GROUPS, GROUP])

        def load_scales(scale_pool, scales, first):
            for r in range(SCALE_ROWS):
                nc.sync.dma_start(
                    out=scale_pool[first + r : P : QUADRANT, :].bitcast(I32),
                    in_=scales[0, r : FEATURES // QUADRANT : SCALE_ROWS, :].bitcast(I32),
                )

        def load_words(word_pool, words):
            nc.sync.dma_start(out=word_pool[:], in_=words[0].rearrange("p n t -> p (n t)").bitcast(I32))

        def load_rows(raw, rows):
            nc.sync.dma_start(out=raw[:], in_=rows.rearrange("(p j) q -> p j q", j=PACK))

        def round_rows(grouped, raw):
            nc.scalar.copy(out=grouped[:], in_=raw[:].rearrange("p j q -> p q j"))

        def quantise(codes, scales, grouped):
            nc.vector.quantize_mx(out=codes[:].bitcast(FP8X4), scales=scales[:], in_=grouped[:].rearrange("p q j -> p (q j)"))

        def gather_words(picked, word_pool, h):
            nc.vector.tensor_copy(out=picked, in_=word_pool[:].bitcast(U32).indirect(half_of(offsets, h, HALF // LIST_ROWS)))

        def product(name, codes, scales, picked, picked_scales):
            acc = ps.tile([P, HALF], F32, name=name)
            nc.tensor.matmul_mx(
                out=acc[:],
                lhsT=codes[:].bitcast(FP8X4),
                lhsT_scale=scales[:],
                rhs=picked.bitcast(FP8X4),
                rhs_scale=picked_scales,
                start=True,
                stop=True,
            )
            return acc

        offsets = tile("offsets", [P, SLOTS // LIST_ROWS], U16)
        key_pool = tile("key_pool", [P, TOKENS], I32)
        val_pool = tile("val_pool", [P, TOKENS], I32)
        key_scale_pool = tile("key_scale_pool", [P, TOKENS], U8)
        val_scale_pool = tile("val_scale_pool", [P, TOKENS], U8)
        query_raw = tile("query_raw", [P, PACK, ROWS], F32)
        th_col = tile("th_col", [P, 1], F32)
        gout_raw = tile("gout_raw", [P, PACK, ROWS], F32)
        base_sb = tile("base_sb", [P, SLOTS], F32)

        nc.vector.memset(key_scale_pool[:].bitcast(I32), 0)
        nc.vector.memset(val_scale_pool[:].bitcast(I32), 0)

        nc.sync.dma_start(offsets[:], offs)
        load_rows(query_raw, query)
        load_scales(key_scale_pool, keys_scales, 0)
        load_words(key_pool, keys_words)
        nc.sync.dma_start(out=th_col[:], in_=th)
        load_scales(val_scale_pool, vals_scales, VAL_SCALE_FIRST)
        load_rows(gout_raw, gout)
        load_words(val_pool, vals_words)
        nc.sync.dma_start(out=base_sb[:], in_=base)

        expo = [tile("expo%d" % h, [P, HALF_GROUPS, PITCH], F32) for h in halves]
        for h in halves:
            nc.scalar.activation(out=expo[h][:, :, GROUP], in_=th_col[:].to_broadcast([P, HALF_GROUPS]), func=ACT.Exp)
        query_bf16 = tile("query_bf16", [P, ROWS, PACK], BF16)
        round_rows(query_bf16, query_raw)

        key_scales = tile("key_scales", [P, SLOTS], U8)
        nc.vector.tensor_copy(out=key_scales[:], in_=key_scale_pool[:].indirect(offsets[:]))
        key_words = tile("key_words", [P, SLOTS], U32)
        query_codes = tile("query_codes", [P, ROWS], U32)
        query_scales = tile("query_scales", [P, ROWS], U8)
        quantise(query_codes, query_scales, query_bf16)
        for h in halves:
            gather_words(half_of(key_words, h), key_pool, h)
        score = [product("score%d" % h, query_codes, query_scales, half_of(key_words, h), half_of(key_scales, h)) for h in halves]

        for h in halves:
            nc.scalar.activation(out=expo[h][:, :, :GROUP], in_=by_group(score[h]), func=ACT.Exp)
        gout_bf16 = tile("gout_bf16", [P, ROWS, PACK], BF16)
        round_rows(gout_bf16, gout_raw)

        val_scales = tile("val_scales", [P, SLOTS], U8)
        nc.vector.tensor_copy(out=val_scales[:], in_=val_scale_pool[:].indirect(offsets[:]))

        denom_all = tile("denom_all", [P, SLOTS // GROUP], F32, "val_scale_pool")
        denom = [half_of(denom_all, h, HALF_GROUPS) for h in halves]
        inv = per_group("inv")
        for h in halves:
            nc.vector.tensor_reduce(out=denom[h][:], in_=expo[h][:, :, : GROUP + 1], axis=AX.X, op=ALU.add)
        for h in halves:
            nc.vector.reciprocal(out=inv[h][:], in_=denom[h][:])

        share = [tile("share0", [P, HALF], F32)]
        nc.vector.tensor_tensor(out=by_group(share[0]), in0=expo[0][:, :, :GROUP], in1=spread(inv[0]), op=ALU.mult)

        gout_codes = tile("gout_codes", [P, ROWS], U32)
        gout_scales = tile("gout_scales", [P, ROWS], U8)
        quantise(gout_codes, gout_scales, gout_bf16)
        val_words = [tile("val_words%d" % h, [P, HALF], U32) for h in halves]
        for h in halves:
            gather_words(val_words[h][:], val_pool, h)
        c = [product("c%d" % h, gout_codes, gout_scales, val_words[h][:], half_of(val_scales, h)[VAL_SCALE_FIRST:P, :]) for h in halves]

        share.append(tile("share1", [P, HALF], F32, "val_pool"))
        nc.vector.tensor_tensor(out=by_group(share[1]), in0=expo[1][:, :, :GROUP], in1=spread(inv[1]), op=ALU.mult)

        share_c, grad, share_grad = per_slot("share_c"), per_slot("grad"), per_slot("share_grad")
        centred, grad_sq, with_base = per_slot("centred"), per_slot("grad_sq"), per_slot("with_base")
        sum_share_c, sum_share_grad, sum_grad_sq = per_group("sum_share_c"), per_group("sum_share_grad"), per_group("sum_grad_sq")
        grad_term, share_term, partial, result = per_slot("grad_term"), per_slot("share_term"), per_slot("partial"), per_slot("result")

        for h in halves:
            nc.vector.tensor_tensor(out=share_c[h][:], in0=c[h][:], in1=share[h][:], op=ALU.mult)
        for h in halves:
            nc.vector.tensor_reduce(out=sum_share_c[h][:], in_=by_group(share_c[h]), axis=AX.X, op=ALU.add)
        for h in halves:
            nc.vector.tensor_tensor(out=by_group(centred[h]), in0=by_group(c[h]), in1=spread(sum_share_c[h]), op=ALU.subtract)
        for h in halves:
            nc.vector.scalar_tensor_tensor(
                out=grad[h][:], in0=centred[h][:], scalar=math.sqrt(PENALTY), in1=share[h][:], op0=ALU.mult, op1=ALU.mult
            )

        for h in halves:
            nc.scalar.activation(out=grad_sq[h][:], in_=grad[h][:], func=ACT.Square)
            nc.vector.tensor_tensor(out=share_grad[h][:], in0=grad[h][:], in1=share[h][:], op=ALU.mult)
        for h in halves:
            nc.vector.tensor_reduce(out=sum_share_grad[h][:], in_=by_group(share_grad[h]), axis=AX.X, op=ALU.add)
        for h in halves:
            nc.vector.tensor_reduce(out=sum_grad_sq[h][:], in_=by_group(grad_sq[h]), axis=AX.X, op=ALU.add)

        for h in halves:
            nc.vector.tensor_tensor(out=with_base[h][:], in0=grad_sq[h][:], in1=half_of(base_sb, h), op=ALU.add)
        for h in halves:
            nc.vector.tensor_tensor(out=by_group(grad_term[h]), in0=by_group(grad[h]), in1=spread(sum_share_grad[h]), op=ALU.mult)
        for h in halves:
            nc.vector.tensor_tensor(out=by_group(share_term[h]), in0=by_group(share[h]), in1=spread(sum_grad_sq[h]), op=ALU.mult)
        for h in halves:
            nc.vector.tensor_tensor(out=partial[h][:], in0=with_base[h][:], in1=grad_term[h][:], op=ALU.subtract)
        for h in halves:
            nc.vector.tensor_tensor(out=result[h][:], in0=partial[h][:], in1=share_term[h][:], op=ALU.subtract)
            nc.sync.dma_start(out=half_of(out, h), in_=result[h][:])
